import numpy as np
import ml_dtypes


def mxq(x, axis, fmt="e4m3"):
    dtype, down = {"e4m3": (ml_dtypes.float8_e4m3fn, 7), "e5m2": (ml_dtypes.float8_e5m2, 14)}[fmt]
    v = np.moveaxis(np.asarray(x, np.float32).astype(ml_dtypes.bfloat16).astype(np.float64), axis, -1)
    blocks = v.reshape(v.shape[:-1] + (-1, 32))
    amax = np.abs(blocks).max(-1, keepdims=True)
    byte = np.maximum(np.where(amax > 0, np.frexp(amax)[1] - 1 + 127, 0) - down, 1)
    scale = np.exp2(byte - 127.0)
    codes = (blocks / scale).astype(np.float32).astype(dtype).astype(np.float64)
    return np.moveaxis((codes * scale).reshape(v.shape), -1, axis)


WIDE = False


def mx_kscale(k):
    if not WIDE:
        return np.ones(k)
    levels = np.array([10, -10, 5, -5, 0])
    if k % 512:
        return np.exp2(np.random.permutation(np.resize(levels, k // 32))).repeat(32)
    a = np.empty((k // 512, 16))
    for p in range(k // 512):
        a[p, :8] = np.random.permutation(np.resize(levels, 8))
        for g in range(8):
            far = levels[np.abs(levels - a[p, g]) >= 10]
            a[p, g + 8] = far[np.random.randint(len(far))]
    return np.exp2(a.ravel()).repeat(32)


def f64(x):
    return np.asarray(x).astype(np.float64)


def striped(idx):
    return np.tile(np.asarray(idx).reshape(-1, 16).T, (8, 1)).astype(np.uint16)


def unstriped(offs):
    return offs[:16].T.reshape(-1).astype(np.int64)


E2M1 = np.array([0.0, 0.5, 1.0, 1.5, 2.0, 3.0, 4.0, 6.0, -0.0, -0.5, -1.0, -1.5, -2.0, -3.0, -4.0, -6.0])


def pack_weight(w, fmt):
    k, n = w.shape
    w = f64(np.asarray(w, np.float32).astype(ml_dtypes.bfloat16)).reshape(k // 32, 32, n)
    amax = np.abs(w).max(1)
    if fmt == "e4m3":
        byte = np.frexp(amax)[1] - 1 + 127 - 7
    else:
        mant, ex = np.frexp(amax / 6.0)
        byte = np.where(mant > 0.5, ex, ex - 1) + 127
    byte = np.clip(np.where(amax > 0, byte, 1), 1, 254)
    scaled = (w * np.exp2(127.0 - byte)[:, None, :]).reshape(k, n).astype(np.float32)
    by_word = np.ascontiguousarray(scaled.reshape(k // 512, 128, 4, n).transpose(0, 1, 3, 2))
    if fmt == "e4m3":
        words = by_word.astype(ml_dtypes.float8_e4m3fn).view(np.uint8)
    else:
        c = by_word.astype(ml_dtypes.float4_e2m1fn).view(np.uint8) & 0xF
        words = (c[..., 0::2] | (c[..., 1::2] << 4)).reshape(k // 512, 128, 2 * n)
    return np.ascontiguousarray(words), np.ascontiguousarray(byte.astype(np.uint8).reshape(k // 512, 16, n))


def unpack_weight(words, scales, fmt):
    g, _, n = scales.shape
    words = np.ascontiguousarray(words).reshape(g, 128, n, -1)
    if fmt == "e4m3":
        vals = words.view(ml_dtypes.float8_e4m3fn).astype(np.float64)
    else:
        nib = np.empty((g, 128, n, 4), np.uint8)
        nib[..., 0::2] = words & 0xF
        nib[..., 1::2] = words >> 4
        vals = E2M1[nib]
    vals = vals * np.repeat(np.exp2(scales.astype(np.float64) - 127.0), 8, axis=1)[..., None]
    return vals.transpose(0, 1, 3, 2).reshape(g * 512, n)


K, R, F, T, J, M = 512, 128, 512, 2048, 512, 256


def setup_inputs():
    n = np.random.standard_normal
    idx = np.random.permutation(T)[:J]
    idx2 = np.random.permutation(J)[:M]
    idx3 = np.random.permutation(J)[:M]
    fk = mx_kscale(K)
    dtabp = pack_weight(n((K, T)) / fk[:, None], "e2m1")
    tabp = pack_weight(n((K, T)) / fk[:, None], "e2m1")
    return {
        "dtab_words": dtabp[0],
        "dtab_scales": dtabp[1],
        "tab_words": tabp[0],
        "tab_scales": tabp[1],
        "w1": (n((K, R)) * 1 / np.sqrt(K) * fk[:, None]).astype(np.float32),
        "soft": (np.random.uniform(0.5, 1.5, (R, 1))).astype(np.float32),
        "og": (np.random.uniform(0.5, 2.0, (R, 1))).astype(np.float32),
        "base": (0.3 * n((R, M))).astype(np.float32),
        "offs": striped(idx),
        "offs2": striped(idx2),
        "offs3": striped(idx3),
    }


def reference(dtab_words, dtab_scales, tab_words, tab_scales, w1, soft, og, base, offs, offs2, offs3):
    idx = unstriped(offs)
    idx2 = unstriped(offs2)
    idx3 = unstriped(offs3)
    dtabu = unpack_weight(dtab_words, dtab_scales, "e2m1")
    tabu = unpack_weight(tab_words, tab_scales, "e2m1")
    w1q = mxq(f64(w1), 0, "e4m3")
    tabidxg = tabu[:, idx]
    a = w1q.T @ tabidxg
    dtabidxg = dtabu[:, idx]
    ta = w1q.T @ dtabidxg
    n2 = np.sqrt(np.square(a[:, idx2]) * np.square(a[:, idx3]) + f64(soft))
    tn2 = (ta[:, idx2] * a[:, idx2] * 2.0 * np.square(a[:, idx3]) + ta[:, idx3] * a[:, idx3] * 2.0 * np.square(a[:, idx2])) * 0.5 / n2
    tu1 = (ta[:, idx2] * a[:, idx3] + ta[:, idx3] * a[:, idx2] - tn2 * a[:, idx2] * a[:, idx3] / n2) / n2
    y = tu1 * f64(og) + f64(base)
    return y

@@ -1,0 +1,135 @@
+from contextlib import ExitStack
+
+import concourse.mybir as mybir
+
+K, R, T, J, M = 512, 128, 2048, 512, 256
+FLOPS = 2 * 2 * K * R * J
+
+F32 = mybir.dt.float32
+BF16 = mybir.dt.bfloat16
+I32 = mybir.dt.int32
+U32 = mybir.dt.uint32
+U16 = mybir.dt.uint16
+U8 = mybir.dt.uint8
+FP8X4 = mybir.dt.float8_e4m3fn_x4
+FP4X4 = mybir.dt.float4_e2m1fn_x4
+ALU = mybir.AluOpType
+ACT = mybir.ActivationFunctionType
+
+P = 128
+PACK = 4
+QUADRANT = 32
+
+
+def load_scale_rows(queue, plane, scales):
+    rows = scales[0].bitcast(I32)
+    for i in range(PACK):
+        queue.dma_start(out=plane[:].bitcast(I32)[i:P:QUADRANT, :], in_=rows[i : 16 : PACK, :])
+
+
+def tile_attend_tlikeness_kernel(
+    tc, dtab_words, dtab_scales, tab_words, tab_scales, w1, soft, og, base, offs, offs2, offs3, out
+):
+    nc = tc.nc
+    with ExitStack() as ctx:
+        pool = ctx.enter_context(tc.tile_pool(name="held", bufs=1))
+        psum = ctx.enter_context(tc.psum_pool(name="psum", bufs=1))
+
+        slots = pool.tile([P, J // 16], U16)
+        first = pool.tile([P, M // 16], U16)
+        second = pool.tile([P, M // 16], U16)
+        tab_w = pool.tile([P, T], U16, align_bytes=64)
+        dtab_w = pool.tile([P, T], U16, align_bytes=64)
+        tab_s = pool.tile([P, T], U8, align_bytes=64)
+        dtab_s = pool.tile([P, T], U8, align_bytes=64)
+        w_raw = pool.tile([P, PACK, R], F32)
+        soft_sb = pool.tile([P, 1], F32)
+        og_sb = pool.tile([P, 1], F32)
+        base_sb = pool.tile([P, M], F32)
+
+        nc.vector.memset(tab_s[:].bitcast(I32), 0)
+        nc.vector.memset(dtab_s[:].bitcast(I32), 0)
+
+        nc.scalar.dma_start(out=tab_w[:].bitcast(I32), in_=tab_words[0].bitcast(I32))
+        nc.sync.dma_start(slots[:], offs)
+        nc.scalar.dma_start(out=dtab_w[:].bitcast(I32), in_=dtab_words[0].bitcast(I32))
+        nc.sync.dma_start(first[:], offs2)
+        nc.scalar.dma_start(out=w_raw[:], in_=w1.rearrange("(p t) r -> p t r", t=PACK))
+        nc.sync.dma_start(second[:], offs3)
+        load_scale_rows(nc.sync, tab_s, tab_scales)
+        load_scale_rows(nc.sync, dtab_s, dtab_scales)
+
+        warm_in = pool.tile([P, 1], F32)
+        warm_out = pool.tile([P, 1], F32)
+        nc.gpsimd.memset(warm_in[:], 1.0)
+        nc.scalar.activation(warm_out[:], warm_in[:], ACT.Abs_reciprocal_sqrt)
+        nc.gpsimd.dma_start(out=soft_sb[:], in_=soft)
+        nc.gpsimd.dma_start(out=og_sb[:], in_=og)
+        nc.gpsimd.dma_start(out=base_sb[:], in_=base)
+
+        w_bf = pool.tile([P, R, PACK], BF16, align_bytes=64)
+        nc.scalar.copy(out=w_bf[:], in_=w_raw[:].rearrange("p t r -> p r t"))
+
+        tab_gs = pool.tile([P, J], U8, align_bytes=64)
+        tab_gw = pool.tile([P, J], U16, align_bytes=64)
+        dtab_gs = pool.tile([P, J], U8, align_bytes=64)
+        dtab_gw = pool.tile([P, J], U16, align_bytes=64)
+        w_codes = pool.tile([P, R], U32, align_bytes=64)
+        w_scales = pool.tile([P, R], U8, align_bytes=64)
+
+        nc.vector.tensor_copy(tab_gw[:], tab_w[:].indirect(slots[:]))
+        nc.vector.tensor_copy(dtab_gw[:], dtab_w[:].indirect(slots[:]))
+        nc.vector.tensor_copy(tab_gs[:], tab_s[:].indirect(slots[:]))
+        nc.vector.quantize_mx(
+            out=w_codes[:].bitcast(FP8X4), scales=w_scales[:], in_=w_bf[:].rearrange("p r t -> p (r t)")
+        )
+        nc.vector.tensor_copy(dtab_gs[:], dtab_s[:].indirect(slots[:]))
+
+        a = pool.tile([R, J], F32)
+        ta = pool.tile([R, J], F32)
+        for name, words, scales, dest in (("a", tab_gw, tab_gs, a), ("ta", dtab_gw, dtab_gs, ta)):
+            for h in range(2):
+                cols = slice(h * J // 2, (h + 1) * J // 2)
+                bank = psum.tile([R, J // 2], F32, name=f"{name}_bank{h}")
+                nc.tensor.matmul_mx(
+                    out=bank[:], lhsT=w_codes[:].bitcast(FP8X4), lhsT_scale=w_scales[:],
+                    rhs=words[:, cols].bitcast(FP4X4), rhs_scale=scales[:, cols], start=True, stop=True,
+                )
+                nc.scalar.copy(out=dest[:, cols], in_=bank[:])
+
+        x = pool.tile([R, M], F32)
+        y = pool.tile([R, M], F32)
+        nc.vector.tensor_copy(x[:], a[:].indirect(first[:]))
+        nc.vector.tensor_copy(y[:], a[:].indirect(second[:]))
+        gain = pool.tile([R, 1], F32)
+        nc.vector.tensor_tensor(gain[:], soft_sb[:], og_sb[:], ALU.mult)
+        xy = pool.tile([R, M], F32)
+        nc.vector.tensor_tensor(xy[:], x[:], y[:], ALU.mult)
+        half = M // 2
+        halves = [slice(h * half, (h + 1) * half) for h in range(2)]
+        xy_sq = pool.tile([R, M], F32)
+        inv_n = pool.tile([R, M], F32)
+        inv_n2 = pool.tile([R, M], F32)
+        for cols in halves:
+            nc.scalar.activation(xy_sq[:, cols], xy[:, cols], ACT.Square)
+        for cols in halves:
+            nc.scalar.activation(inv_n[:, cols], xy_sq[:, cols], ACT.Abs_reciprocal_sqrt, bias=soft_sb[:])
+        for cols in halves:
+            nc.scalar.activation(inv_n2[:, cols], inv_n[:, cols], ACT.Square)
+
+        x_ty = pool.tile([R, M], F32)
+        tx_y = pool.tile([R, M], F32)
+        nc.vector.tensor_tensor(x_ty[:], ta[:].indirect(second[:]), x[:], ALU.mult)
+        nc.vector.tensor_tensor(tx_y[:], ta[:].indirect(first[:]), y[:], ALU.mult)
+        slope = pool.tile([R, M], F32)
+        nc.vector.scalar_tensor_tensor(slope[:], inv_n[:], gain[:], inv_n2[:], ALU.mult, ALU.mult)
+        txy = pool.tile([R, M], F32)
+        change = pool.tile([R, M], F32)
+        result = pool.tile([R, M], F32)
+        for cols in halves:
+            nc.vector.tensor_tensor(txy[:, cols], x_ty[:, cols], tx_y[:, cols], ALU.add)
+        for cols in halves:
+            nc.vector.tensor_tensor(change[:, cols], txy[:, cols], slope[:, cols], ALU.mult)
+        for cols, queue in zip(halves, (nc.sync, nc.scalar)):
+            nc.vector.tensor_tensor(result[:, cols], change[:, cols], base_sb[:, cols], ALU.add)
+            queue.dma_start(out=out[:, cols], in_=result[:, cols])

@@ -23,8 +23,10 @@ QUADRANT = 32
 
 def load_scale_rows(queue, plane, scales):
     rows = scales[0].bitcast(I32)
-    for i in range(PACK):
-        queue.dma_start(out=plane[:].bitcast(I32)[i:P:QUADRANT, :], in_=rows[i : 16 : PACK, :])
+    for q in range(P // QUADRANT):
+        queue.dma_start(
+            out=plane[:].bitcast(I32)[QUADRANT * q : QUADRANT * q + 4, :], in_=rows[4 * q : 4 * q + 4, :]
+        )
 
 
 def tile_attend_tlikeness_kernel(
@@ -40,32 +42,33 @@ def tile_attend_tlikeness_kernel(
         second = pool.tile([P, M // 16], U16)
         tab_w = pool.tile([P, T], U16, align_bytes=64)
         dtab_w = pool.tile([P, T], U16, align_bytes=64)
-        tab_s = pool.tile([P, T], U8, align_bytes=64)
+        tab_s = pool.tile([P, T], U8, align_bytes=64, tag="tab_s_then_w_scales")
         dtab_s = pool.tile([P, T], U8, align_bytes=64)
         w_raw = pool.tile([P, PACK, R], F32)
+
         soft_sb = pool.tile([P, 1], F32)
         og_sb = pool.tile([P, 1], F32)
         base_sb = pool.tile([P, M], F32)
 
-        nc.vector.memset(tab_s[:].bitcast(I32), 0)
-        nc.vector.memset(dtab_s[:].bitcast(I32), 0)
-
-        nc.scalar.dma_start(out=tab_w[:].bitcast(I32), in_=tab_words[0].bitcast(I32))
-        nc.sync.dma_start(slots[:], offs)
-        nc.scalar.dma_start(out=dtab_w[:].bitcast(I32), in_=dtab_words[0].bitcast(I32))
-        nc.sync.dma_start(first[:], offs2)
-        nc.scalar.dma_start(out=w_raw[:], in_=w1.rearrange("(p t) r -> p t r", t=PACK))
-        nc.sync.dma_start(second[:], offs3)
-        load_scale_rows(nc.sync, tab_s, tab_scales)
-        load_scale_rows(nc.sync, dtab_s, dtab_scales)
-
         warm_in = pool.tile([P, 1], F32)
         warm_out = pool.tile([P, 1], F32)
         nc.gpsimd.memset(warm_in[:], 1.0)
+        nc.vector.memset(tab_s[:].bitcast(I32), 0)
+        nc.vector.memset(dtab_s[:].bitcast(I32), 0)
+
+        nc.sync.dma_start(out=tab_w[:].bitcast(I32), in_=tab_words[0].bitcast(I32))
+        nc.sync.dma_start(slots[:], offs)
+        nc.sync.dma_start(out=soft_sb[:], in_=soft)
+        load_scale_rows(nc.sync, tab_s, tab_scales)
+        nc.sync.dma_start(out=w_raw[:], in_=w1.rearrange("(p t) r -> p t r", t=PACK))
+        nc.sync.dma_start(out=dtab_w[:].bitcast(I32), in_=dtab_words[0].bitcast(I32))
+        load_scale_rows(nc.sync, dtab_s, dtab_scales)
+        nc.sync.dma_start(first[:], offs2)
+        nc.sync.dma_start(second[:], offs3)
+        nc.sync.dma_start(out=og_sb[:], in_=og)
+        nc.sync.dma_start(out=base_sb[:], in_=base)
+
         nc.scalar.activation(warm_out[:], warm_in[:], ACT.Abs_reciprocal_sqrt)
-        nc.gpsimd.dma_start(out=soft_sb[:], in_=soft)
-        nc.gpsimd.dma_start(out=og_sb[:], in_=og)
-        nc.gpsimd.dma_start(out=base_sb[:], in_=base)
 
         w_bf = pool.tile([P, R, PACK], BF16, align_bytes=64)
         nc.scalar.copy(out=w_bf[:], in_=w_raw[:].rearrange("p t r -> p r t"))
@@ -75,15 +78,19 @@ def tile_attend_tlikeness_kernel(
         dtab_gs = pool.tile([P, J], U8, align_bytes=64)
         dtab_gw = pool.tile([P, J], U16, align_bytes=64)
         w_codes = pool.tile([P, R], U32, align_bytes=64)
-        w_scales = pool.tile([P, R], U8, align_bytes=64)
 
         nc.vector.tensor_copy(tab_gw[:], tab_w[:].indirect(slots[:]))
-        nc.vector.tensor_copy(dtab_gw[:], dtab_w[:].indirect(slots[:]))
         nc.vector.tensor_copy(tab_gs[:], tab_s[:].indirect(slots[:]))
+        w_scales = pool.tile([P, R], U8, align_bytes=64, tag="tab_s_then_w_scales")
         nc.vector.quantize_mx(
             out=w_codes[:].bitcast(FP8X4), scales=w_scales[:], in_=w_bf[:].rearrange("p r t -> p (r t)")
         )
-        nc.vector.tensor_copy(dtab_gs[:], dtab_s[:].indirect(slots[:]))
+        nc.vector.tensor_copy(dtab_gw[:], dtab_w[:].indirect(slots[:]))
+        for h in range(2):
+            nc.vector.tensor_copy(
+                dtab_gs[:, h * J // 2 : (h + 1) * J // 2],
+                dtab_s[:].indirect(slots[:, h * J // 32 : (h + 1) * J // 32]),
+            )
 
         a = pool.tile([R, J], F32)
         ta = pool.tile([R, J], F32)
@@ -101,12 +108,16 @@ def tile_attend_tlikeness_kernel(
         y = pool.tile([R, M], F32)
         nc.vector.tensor_copy(x[:], a[:].indirect(first[:]))
         nc.vector.tensor_copy(y[:], a[:].indirect(second[:]))
-        gain = pool.tile([R, 1], F32)
-        nc.vector.tensor_tensor(gain[:], soft_sb[:], og_sb[:], ALU.mult)
-        xy = pool.tile([R, M], F32)
-        nc.vector.tensor_tensor(xy[:], x[:], y[:], ALU.mult)
         half = M // 2
         halves = [slice(h * half, (h + 1) * half) for h in range(2)]
+        list_halves = [slice(h * half // 16, (h + 1) * half // 16) for h in range(2)]
+        xy = pool.tile([R, M], F32)
+        x_ty = pool.tile([R, M], F32)
+        tx_y = pool.tile([R, M], F32)
+        nc.vector.tensor_tensor(
+            x_ty[:, halves[0]], ta[:].indirect(second[:, list_halves[0]]), x[:, halves[0]], ALU.mult
+        )
+        nc.vector.tensor_tensor(xy[:], x[:], y[:], ALU.mult)
         xy_sq = pool.tile([R, M], F32)
         inv_n = pool.tile([R, M], F32)
         inv_n2 = pool.tile([R, M], F32)
@@ -117,19 +128,25 @@ def tile_attend_tlikeness_kernel(
         for cols in halves:
             nc.scalar.activation(inv_n2[:, cols], inv_n[:, cols], ACT.Square)
 
-        x_ty = pool.tile([R, M], F32)
-        tx_y = pool.tile([R, M], F32)
-        nc.vector.tensor_tensor(x_ty[:], ta[:].indirect(second[:]), x[:], ALU.mult)
-        nc.vector.tensor_tensor(tx_y[:], ta[:].indirect(first[:]), y[:], ALU.mult)
-        slope = pool.tile([R, M], F32)
-        nc.vector.scalar_tensor_tensor(slope[:], inv_n[:], gain[:], inv_n2[:], ALU.mult, ALU.mult)
+        nc.vector.tensor_tensor(
+            x_ty[:, halves[1]], ta[:].indirect(second[:, list_halves[1]]), x[:, halves[1]], ALU.mult
+        )
+        for cols, entries in zip(halves, list_halves):
+            nc.vector.tensor_tensor(tx_y[:, cols], ta[:].indirect(first[:, entries]), y[:, cols], ALU.mult)
         txy = pool.tile([R, M], F32)
+        once = pool.tile([R, M], F32)
         change = pool.tile([R, M], F32)
         result = pool.tile([R, M], F32)
         for cols in halves:
             nc.vector.tensor_tensor(txy[:, cols], x_ty[:, cols], tx_y[:, cols], ALU.add)
         for cols in halves:
-            nc.vector.tensor_tensor(change[:, cols], txy[:, cols], slope[:, cols], ALU.mult)
+            nc.vector.scalar_tensor_tensor(
+                once[:, cols], txy[:, cols], soft_sb[:], inv_n[:, cols], ALU.mult, ALU.mult
+            )
+        for cols in halves:
+            nc.vector.tensor_tensor(change[:, cols], once[:, cols], inv_n2[:, cols], ALU.mult)
         for cols, queue in zip(halves, (nc.sync, nc.scalar)):
-            nc.vector.tensor_tensor(result[:, cols], change[:, cols], base_sb[:, cols], ALU.add)
+            nc.vector.scalar_tensor_tensor(
+                result[:, cols], change[:, cols], og_sb[:], base_sb[:, cols], ALU.mult, ALU.add
+            )
             queue.dma_start(out=out[:, cols], in_=result[:, cols])

from contextlib import ExitStack

import concourse.mybir as mybir

K, R, T, J, M = 512, 128, 2048, 512, 256
FLOPS = 2 * 2 * K * R * J

F32 = mybir.dt.float32
BF16 = mybir.dt.bfloat16
I32 = mybir.dt.int32
U32 = mybir.dt.uint32
U16 = mybir.dt.uint16
U8 = mybir.dt.uint8
FP8X4 = mybir.dt.float8_e4m3fn_x4
FP4X4 = mybir.dt.float4_e2m1fn_x4
ALU = mybir.AluOpType
ACT = mybir.ActivationFunctionType

P = 128
PACK = 4
QUADRANT = 32


def load_scale_rows(queue, plane, scales):
    rows = scales[0].bitcast(I32)
    for q in range(P // QUADRANT):
        queue.dma_start(
            out=plane[:].bitcast(I32)[QUADRANT * q : QUADRANT * q + 4, :], in_=rows[4 * q : 4 * q + 4, :]
        )


def tile_attend_tlikeness_kernel(
    tc, dtab_words, dtab_scales, tab_words, tab_scales, w1, soft, og, base, offs, offs2, offs3, out
):
    nc = tc.nc
    with ExitStack() as ctx:
        pool = ctx.enter_context(tc.tile_pool(name="held", bufs=1))
        psum = ctx.enter_context(tc.psum_pool(name="psum", bufs=1))

        slots = pool.tile([P, J // 16], U16)
        first = pool.tile([P, M // 16], U16)
        second = pool.tile([P, M // 16], U16)
        tab_w = pool.tile([P, T], U16, align_bytes=64)
        dtab_w = pool.tile([P, T], U16, align_bytes=64)
        tab_s = pool.tile([P, T], U8, align_bytes=64, tag="tab_s_then_w_scales")
        dtab_s = pool.tile([P, T], U8, align_bytes=64)
        w_raw = pool.tile([P, PACK, R], F32)

        soft_sb = pool.tile([P, 1], F32)
        og_sb = pool.tile([P, 1], F32)
        base_sb = pool.tile([P, M], F32)

        warm_in = pool.tile([P, 1], F32)
        warm_out = pool.tile([P, 1], F32)
        nc.gpsimd.memset(warm_in[:], 1.0)
        nc.vector.memset(tab_s[:].bitcast(I32), 0)
        nc.vector.memset(dtab_s[:].bitcast(I32), 0)

        nc.sync.dma_start(out=tab_w[:].bitcast(I32), in_=tab_words[0].bitcast(I32))
        nc.sync.dma_start(slots[:], offs)
        nc.sync.dma_start(out=soft_sb[:], in_=soft)
        load_scale_rows(nc.sync, tab_s, tab_scales)
        nc.sync.dma_start(out=w_raw[:], in_=w1.rearrange("(p t) r -> p t r", t=PACK))
        nc.sync.dma_start(out=dtab_w[:].bitcast(I32), in_=dtab_words[0].bitcast(I32))
        load_scale_rows(nc.sync, dtab_s, dtab_scales)
        nc.sync.dma_start(first[:], offs2)
        nc.sync.dma_start(second[:], offs3)
        nc.sync.dma_start(out=og_sb[:], in_=og)
        nc.sync.dma_start(out=base_sb[:], in_=base)

        nc.scalar.activation(warm_out[:], warm_in[:], ACT.Abs_reciprocal_sqrt)

        w_bf = pool.tile([P, R, PACK], BF16, align_bytes=64)
        nc.scalar.copy(out=w_bf[:], in_=w_raw[:].rearrange("p t r -> p r t"))

        tab_gs = pool.tile([P, J], U8, align_bytes=64)
        tab_gw = pool.tile([P, J], U16, align_bytes=64)
        dtab_gs = pool.tile([P, J], U8, align_bytes=64)
        dtab_gw = pool.tile([P, J], U16, align_bytes=64)
        w_codes = pool.tile([P, R], U32, align_bytes=64)

        nc.vector.tensor_copy(tab_gw[:], tab_w[:].indirect(slots[:]))
        nc.vector.tensor_copy(tab_gs[:], tab_s[:].indirect(slots[:]))
        w_scales = pool.tile([P, R], U8, align_bytes=64, tag="tab_s_then_w_scales")
        nc.vector.quantize_mx(
            out=w_codes[:].bitcast(FP8X4), scales=w_scales[:], in_=w_bf[:].rearrange("p r t -> p (r t)")
        )
        nc.vector.tensor_copy(dtab_gw[:], dtab_w[:].indirect(slots[:]))
        for h in range(2):
            nc.vector.tensor_copy(
                dtab_gs[:, h * J // 2 : (h + 1) * J // 2],
                dtab_s[:].indirect(slots[:, h * J // 32 : (h + 1) * J // 32]),
            )

        a = pool.tile([R, J], F32)
        ta = pool.tile([R, J], F32)
        for name, words, scales, dest in (("a", tab_gw, tab_gs, a), ("ta", dtab_gw, dtab_gs, ta)):
            for h in range(2):
                cols = slice(h * J // 2, (h + 1) * J // 2)
                bank = psum.tile([R, J // 2], F32, name=f"{name}_bank{h}")
                nc.tensor.matmul_mx(
                    out=bank[:], lhsT=w_codes[:].bitcast(FP8X4), lhsT_scale=w_scales[:],
                    rhs=words[:, cols].bitcast(FP4X4), rhs_scale=scales[:, cols], start=True, stop=True,
                )
                nc.scalar.copy(out=dest[:, cols], in_=bank[:])

        x = pool.tile([R, M], F32)
        y = pool.tile([R, M], F32)
        nc.vector.tensor_copy(x[:], a[:].indirect(first[:]))
        nc.vector.tensor_copy(y[:], a[:].indirect(second[:]))
        half = M // 2
        halves = [slice(h * half, (h + 1) * half) for h in range(2)]
        list_halves = [slice(h * half // 16, (h + 1) * half // 16) for h in range(2)]
        xy = pool.tile([R, M], F32)
        x_ty = pool.tile([R, M], F32)
        tx_y = pool.tile([R, M], F32)
        nc.vector.tensor_tensor(
            x_ty[:, halves[0]], ta[:].indirect(second[:, list_halves[0]]), x[:, halves[0]], ALU.mult
        )
        nc.vector.tensor_tensor(xy[:], x[:], y[:], ALU.mult)
        xy_sq = pool.tile([R, M], F32)
        inv_n = pool.tile([R, M], F32)
        inv_n2 = pool.tile([R, M], F32)
        for cols in halves:
            nc.scalar.activation(xy_sq[:, cols], xy[:, cols], ACT.Square)
        for cols in halves:
            nc.scalar.activation(inv_n[:, cols], xy_sq[:, cols], ACT.Abs_reciprocal_sqrt, bias=soft_sb[:])
        for cols in halves:
            nc.scalar.activation(inv_n2[:, cols], inv_n[:, cols], ACT.Square)

        nc.vector.tensor_tensor(
            x_ty[:, halves[1]], ta[:].indirect(second[:, list_halves[1]]), x[:, halves[1]], ALU.mult
        )
        for cols, entries in zip(halves, list_halves):
            nc.vector.tensor_tensor(tx_y[:, cols], ta[:].indirect(first[:, entries]), y[:, cols], ALU.mult)
        txy = pool.tile([R, M], F32)
        once = pool.tile([R, M], F32)
        change = pool.tile([R, M], F32)
        result = pool.tile([R, M], F32)
        for cols in halves:
            nc.vector.tensor_tensor(txy[:, cols], x_ty[:, cols], tx_y[:, cols], ALU.add)
        for cols in halves:
            nc.vector.scalar_tensor_tensor(
                once[:, cols], txy[:, cols], soft_sb[:], inv_n[:, cols], ALU.mult, ALU.mult
            )
        for cols in halves:
            nc.vector.tensor_tensor(change[:, cols], once[:, cols], inv_n2[:, cols], ALU.mult)
        for cols, queue in zip(halves, (nc.sync, nc.scalar)):
            nc.vector.scalar_tensor_tensor(
                result[:, cols], change[:, cols], og_sb[:], base_sb[:, cols], ALU.mult, ALU.add
            )
            queue.dma_start(out=out[:, cols], in_=result[:, cols])
